import numpy as np
import ml_dtypes


def mxq(x, axis, fmt="e4m3"):
    dtype, down = {"e4m3": (ml_dtypes.float8_e4m3fn, 7), "e5m2": (ml_dtypes.float8_e5m2, 14)}[fmt]
    v = np.moveaxis(np.asarray(x, np.float32).astype(ml_dtypes.bfloat16).astype(np.float64), axis, -1)
    blocks = v.reshape(v.shape[:-1] + (-1, 32))
    amax = np.abs(blocks).max(-1, keepdims=True)
    byte = np.maximum(np.where(amax > 0, np.frexp(amax)[1] - 1 + 127, 0) - down, 1)
    scale = np.exp2(byte - 127.0)
    codes = (blocks / scale).astype(np.float32).astype(dtype).astype(np.float64)
    return np.moveaxis((codes * scale).reshape(v.shape), -1, axis)


WIDE = False


def mx_kscale(k):
    if not WIDE:
        return np.ones(k)
    levels = np.array([10, -10, 5, -5, 0])
    if k % 512:
        return np.exp2(np.random.permutation(np.resize(levels, k // 32))).repeat(32)
    a = np.empty((k // 512, 16))
    for p in range(k // 512):
        a[p, :8] = np.random.permutation(np.resize(levels, 8))
        for g in range(8):
            far = levels[np.abs(levels - a[p, g]) >= 10]
            a[p, g + 8] = far[np.random.randint(len(far))]
    return np.exp2(a.ravel()).repeat(32)


def f64(x):
    return np.asarray(x).astype(np.float64)


def striped(idx):
    return np.tile(idx.reshape(-1, 16).T, (8, 1)).astype(np.uint16)


def unstriped(offs):
    return offs[:16].T.reshape(-1).astype(np.int64)


def striped8(idx):
    return np.concatenate([x.reshape(-1, 16).T for x in idx]).astype(np.uint16)


def runs(offs, k):
    lists = np.stack([offs[16 * r : 16 * r + 16].T.reshape(-1) for r in range(8)]).astype(np.int64)
    return lists[np.arange(k) % 512 // 64]


def pack_weight(w):
    k, n = w.shape
    w = f64(np.asarray(w, np.float32).astype(ml_dtypes.bfloat16)).reshape(k // 32, 32, n)
    amax = np.abs(w).max(1)
    byte = np.clip(np.where(amax > 0, np.frexp(amax)[1] - 1 + 127 - 7, 1), 1, 254)
    scaled = (w * np.exp2(127.0 - byte)[:, None, :]).reshape(k, n).astype(np.float32)
    words = np.ascontiguousarray(scaled.reshape(k // 512, 128, 4, n).transpose(0, 1, 3, 2)).astype(ml_dtypes.float8_e4m3fn).view(np.uint8)
    return words, np.ascontiguousarray(byte.astype(np.uint8).reshape(k // 512, 16, n))


def unpack_weight(words, scales):
    g, p, n, _ = words.shape
    vals = np.ascontiguousarray(words).view(ml_dtypes.float8_e4m3fn).astype(np.float64) * np.repeat(np.exp2(scales.astype(np.float64) - 127.0), 8, axis=1)[..., None]
    return vals.transpose(0, 1, 3, 2).reshape(g * 512, n)


E2M1 = np.array([0.0, 0.5, 1.0, 1.5, 2.0, 3.0, 4.0, 6.0, -0.0, -0.5, -1.0, -1.5, -2.0, -3.0, -4.0, -6.0])


def pack_fp4(w):
    k, n = w.shape
    w = f64(np.asarray(w, np.float32).astype(ml_dtypes.bfloat16)).reshape(k // 32, 32, n)
    amax = np.abs(w).max(1)
    mant, ex = np.frexp(amax / 6.0)
    byte = np.clip(np.where(amax > 0, np.where(mant > 0.5, ex, ex - 1) + 127, 1), 1, 254)
    scaled = (w * np.exp2(127.0 - byte)[:, None, :]).reshape(k, n).astype(np.float32)
    c = np.ascontiguousarray(scaled.reshape(k // 512, 128, 4, n).transpose(0, 1, 3, 2)).astype(ml_dtypes.float4_e2m1fn).view(np.uint8) & 0xF
    words = (c[..., 0::2] | (c[..., 1::2] << 4)).reshape(k // 512, 128, 2 * n)
    return np.ascontiguousarray(words), np.ascontiguousarray(byte.astype(np.uint8).reshape(k // 512, 16, n))


def unpack_fp4(words, scales):
    g, _, n = scales.shape
    words = np.ascontiguousarray(words).reshape(g, 128, n, 2)
    nib = np.empty((g, 128, n, 4), np.uint8)
    nib[..., 0::2] = words & 0xF
    nib[..., 1::2] = words >> 4
    vals = E2M1[nib] * np.repeat(np.exp2(scales.astype(np.float64) - 127.0), 8, axis=1)[..., None]
    return vals.transpose(0, 1, 3, 2).reshape(g * 512, n)


def planes(y):
    n, m = y.shape
    v = y.astype(np.float32).astype(ml_dtypes.bfloat16).astype(np.float64).reshape(n // 32, 32, m)
    top = np.abs(v).max(1)
    byte = np.clip(np.where(top > 0, np.frexp(top)[1] - 1 + 127 - 7, 1), 1, 254)
    codes = (v * np.exp2(127.0 - byte)[:, None, :]).reshape(n, m).astype(np.float32).astype(ml_dtypes.float8_e4m3fn).view(np.uint8)
    words = codes.reshape(n // 512, 128, 4, m).transpose(0, 1, 3, 2)
    return np.ascontiguousarray(words), np.ascontiguousarray(byte.astype(np.uint8).reshape(n // 512, 16, m))


K, T, S, N, H, J = 512, 2048, 512, 512, 512, 512


def setup_inputs():
    n = np.random.standard_normal
    s = mx_kscale(K)[:, None]
    u = mx_kscale(S)
    packed_xT = pack_weight(n((K, T)) * s)
    packed_w1 = pack_fp4(n((S, N)) / np.sqrt(S) / u[:, None])
    return {
        "x_words": packed_xT[0],
        "x_scales": packed_xT[1],
        "wa": (n((K, H)) / np.sqrt(K) / s).astype(np.float32),
        "tab": n((S, J)).astype(np.float32),
        "gt": (np.random.uniform(0.5, 1.5, (S, 1)) * u[:, None]).astype(np.float32),
        "w1_words": packed_w1[0],
        "w1_scales": packed_w1[1],
        "offs": striped(np.random.permutation(T)[:S]),
        "n1": striped8(np.random.randint(0, J, (8, H))),
        "n2": striped8(np.random.randint(0, J, (8, H))),
        "n3": striped8(np.stack([np.random.permutation(H) for _ in range(8)])),
        "n4": striped8(np.stack([np.random.permutation(H) for _ in range(8)])),
    }


def reference(x_words, x_scales, wa, tab, gt, w1_words, w1_scales, offs, n1, n2, n3, n4):
    xq = unpack_weight(x_words, x_scales)[:, unstriped(offs)]
    y = xq.T @ mxq(f64(wa), 0, "e4m3")
    z = f64(gt) * ((y[np.arange(S)[:, None], runs(n3, S)]) * (f64(tab)[np.arange(S)[:, None], runs(n1, S)]) + f64(tab)[np.arange(S)[:, None], runs(n2, S)])
    h = unpack_fp4(w1_words, w1_scales).T @ mxq(z, 0, "e4m3")
    out_0 = h - (h[np.arange(N)[:, None], runs(n4, N)])
    return (out_0,) + planes(out_0)

@@ -1,0 +1,190 @@
+from contextlib import ExitStack
+
+import concourse.mybir as mybir
+
+K, T, S, N, H = 512, 2048, 512, 512, 512
+FLOPS = 2 * K * S * H + 2 * S * N * H
+
+F32 = mybir.dt.float32
+BF16 = mybir.dt.bfloat16
+I32 = mybir.dt.int32
+U32 = mybir.dt.uint32
+U16 = mybir.dt.uint16
+U8 = mybir.dt.uint8
+FP8X4 = mybir.dt.float8_e4m3fn_x4
+FP4X4 = mybir.dt.float4_e2m1fn_x4
+COPY = mybir.ActivationFunctionType.Copy
+MULT = mybir.AluOpType.mult
+ADD = mybir.AluOpType.add
+
+P = 128
+PACK = 4
+HALF = H // 2
+CHUNKS = ((0, 256), (256, 128), (384, 128))
+Z_CHUNK = 128
+
+
+def tile_picked_tokkindadif_none_po_kernel(
+    tc, x_words, x_scales, wa, tab, gt, w1_words, w1_scales, offs, n1, n2, n3, n4, out_0, out_1, out_2
+):
+    nc = tc.nc
+    with ExitStack() as ctx:
+        lists = ctx.enter_context(tc.tile_pool(name="lists", bufs=1))
+        sb = ctx.enter_context(tc.tile_pool(name="sb", bufs=1))
+        ps = ctx.enter_context(tc.psum_pool(name="ps", bufs=1))
+
+        def tile(shape, dtype, name):
+            return sb.tile(shape, dtype, name=name, align_bytes=64)
+
+        def load_list(src, name):
+            dst = lists.tile([P, 32], U16, name=name)
+            nc.sync.dma_start(dst[:], src)
+            return dst
+
+        def entries(lst, start, width):
+            return lst[:, start // 16 : (start + width) // 16]
+
+        def interleave(engine_copy, dst, src):
+            engine_copy(
+                dst[:].rearrange("p (c i t) -> p c t i", i=4, t=PACK),
+                src[:].rearrange("p t (c i) -> p c t i", i=4),
+            )
+
+        xs = tile([P, T], U8, "xs")
+        nc.vector.memset(xs[:].bitcast(I32), 0)
+        w1s = tile([P, N], U8, "w1s")
+        nc.vector.memset(w1s[:].bitcast(I32), 0)
+
+        tab_rows = tab.rearrange("(p t) j -> p t j", t=PACK)
+        wa_rows = wa.rearrange("(p t) j -> p t j", t=PACK)
+        tab_t = [tile([P, H], F32, "tab%d" % t) for t in range(PACK)]
+        wa_raw = [tile([P, PACK, HALF], F32, "wa_raw%d" % u) for u in range(2)]
+        xw = tile([P, T], I32, "xw")
+        gt_t = tile([P, PACK], F32, "gt_t")
+        w1w = tile([P, 2 * N], U8, "w1w")
+
+        n1_t = load_list(n1, "n1_t")
+        for t in (0, 1):
+            nc.sync.dma_start(tab_t[t][:], tab_rows[:, t, :])
+        for u in range(2):
+            nc.sync.dma_start(wa_raw[u][:], wa_rows[:, :, u * HALF : (u + 1) * HALF])
+        offs_t = load_list(offs, "offs_t")
+        nc.sync.dma_start(xw[:], x_words[0].rearrange("p c r -> p (c r)").bitcast(I32))
+        for t in (2, 3):
+            nc.sync.dma_start(tab_t[t][:], tab_rows[:, t, :])
+        n3_t = load_list(n3, "n3_t")
+        n2_t = load_list(n2, "n2_t")
+        n4_t = load_list(n4, "n4_t")
+        nc.sync.dma_start(w1w[:].bitcast(I32), w1_words[0].bitcast(I32))
+        for q in range(4):
+            nc.gpsimd.dma_start(xs[32 * q : 32 * q + 4, :].bitcast(I32), x_scales[0, 4 * q : 4 * q + 4, :].bitcast(I32))
+        nc.gpsimd.dma_start(gt_t[:], gt.rearrange("(p t) o -> p (t o)", t=PACK))
+        for q in range(4):
+            nc.gpsimd.dma_start(w1s[32 * q : 32 * q + 4, :].bitcast(I32), w1_scales[0, 4 * q : 4 * q + 4, :].bitcast(I32))
+
+        a = [tile([P, H], F32, "a%d" % t) for t in range(PACK)]
+        tabg = [tile([P, H], F32, "tabg%d" % t) for t in range(PACK)]
+
+        def fetch_n1(t):
+            for u in range(2):
+                nc.vector.tensor_copy(a[t][:, u * HALF : (u + 1) * HALF], tab_t[t][:].indirect(entries(n1_t, u * HALF, HALF)))
+
+        fetch_n1(0)
+        fetch_n1(1)
+
+        xsg = tile([P, S], U8, "xsg")
+        nc.vector.tensor_copy(xsg[:], xs[:].indirect(offs_t[:]))
+        xsd = tile([P, S], U8, "xsd")
+        nc.vector.tensor_copy(
+            xsd[:].rearrange("p (t c i) -> p c t i", t=PACK, i=16),
+            xsg[:].rearrange("p (c i t) -> p c t i", t=PACK, i=16),
+        )
+        wa_codes = tile([P, H], U32, "wa_codes")
+        wa_scales = tile([P, H], U8, "wa_scales")
+        for u in range(2):
+            grouped = tile([P, PACK * HALF], BF16, "wa_bf%d" % u)
+            interleave(nc.scalar.copy, grouped, wa_raw[u])
+            cols = slice(u * HALF, (u + 1) * HALF)
+            nc.vector.quantize_mx(out=wa_codes[:, cols].bitcast(FP8X4), scales=wa_scales[:, cols], in_=grouped[:])
+        xg = tile([P, S], I32, "xg")
+        nc.vector.tensor_copy(xg[:].bitcast(U32), xw[:].bitcast(U32).indirect(offs_t[:]))
+        xd = tile([P, S], I32, "xd")
+        nc.vector.tensor_copy(
+            xd[:].rearrange("p (t c i) -> p c t i", t=PACK, i=4),
+            xg[:].rearrange("p (c i t) -> p c t i", t=PACK, i=4),
+        )
+        fetch_n1(2)
+        fetch_n1(3)
+
+        y_t = []
+        for t in range(PACK):
+            cols = slice(t * P, (t + 1) * P)
+            bank = ps.tile([P, H], F32, name="ybank%d" % t)
+            nc.tensor.matmul_mx(
+                out=bank[:], lhsT=xd[:, cols].bitcast(FP8X4), lhsT_scale=xsd[:, cols],
+                rhs=wa_codes[:].bitcast(FP8X4), rhs_scale=wa_scales[:], start=True, stop=True,
+            )
+            plane = tile([P, H], F32, "y%d" % t)
+            nc.scalar.activation(plane[:], bank[:], COPY, scale=gt_t[:, t : t + 1])
+            y_t.append(plane)
+
+        for t in range(PACK):
+            nc.scalar.activation(tabg[t][:], tab_t[t][:], COPY, scale=gt_t[:, t : t + 1])
+
+        w1d = tile([P, 2 * N], U8, "w1d")
+        nc.vector.tensor_copy(
+            w1d[:].rearrange("p (t c i b) -> p c t i b", t=PACK, i=8, b=2),
+            w1w[:].rearrange("p (c i t b) -> p c t i b", t=PACK, i=8, b=2),
+        )
+        w1sd = tile([P, N], U8, "w1sd")
+        nc.vector.tensor_copy(
+            w1sd[:].rearrange("p (t c i) -> p c t i", t=PACK, i=16),
+            w1s[:].rearrange("p (c i t) -> p c t i", t=PACK, i=16),
+        )
+
+        hbank = [ps.tile([P, H], F32, name="hbank%d" % t) for t in range(PACK)]
+        neg_h = [tile([P, H], F32, "neg_h%d" % t) for t in range(PACK)]
+        h = [tile([P, H], F32, "h%d" % t) for t in range(PACK)]
+        b = [tile([P, H], F32, "b%d" % t) for t in range(PACK)]
+        width = Z_CHUNK
+        for c, start in enumerate(range(0, H, Z_CHUNK)):
+            cols = slice(start, start + width)
+            z = tile([P, PACK, width], F32, "z%d" % c)
+            if start % HALF == 0:
+                half = slice(start, start + HALF)
+                for t in range(PACK):
+                    nc.vector.tensor_tensor(b[t][:, half], y_t[t][:].indirect(entries(n3_t, start, HALF)), a[t][:, half], MULT)
+            for t in range(PACK):
+                nc.vector.tensor_tensor(z[:, t, :], tabg[t][:].indirect(entries(n2_t, start, width)), b[t][:, cols], ADD)
+            z_bf = tile([P, PACK * width], BF16, "z_bf%d" % c)
+            interleave(nc.vector.tensor_copy if start + width == H else nc.scalar.copy, z_bf, z)
+            z_codes = tile([P, width], U32, "z_codes%d" % c)
+            z_scales = tile([P, width], U8, "z_scales%d" % c)
+            nc.vector.quantize_mx(out=z_codes[:].bitcast(FP8X4), scales=z_scales[:], in_=z_bf[:])
+            for t in range(PACK):
+                nc.tensor.matmul_mx(
+                    out=hbank[t][:, cols], lhsT=w1d[:, 2 * P * t : 2 * P * (t + 1)].bitcast(FP4X4),
+                    lhsT_scale=w1sd[:, P * t : P * (t + 1)],
+                    rhs=z_codes[:].bitcast(FP8X4), rhs_scale=z_scales[:], start=True, stop=True,
+                )
+                nc.scalar.activation(neg_h[t][:, cols], hbank[t][:, cols], COPY, scale=-1.0)
+            for t in range(PACK):
+                nc.scalar.copy(h[t][:, cols], hbank[t][:, cols])
+
+        out_rows = out_0.rearrange("(p t) j -> p t j", t=PACK)
+        out_words = out_1[0].rearrange("p c r -> p (c r)").bitcast(I32)
+        o_scales = tile([P, H], U8, "o_scales")
+        for c, (start, width) in enumerate(CHUNKS):
+            cols = slice(start, start + width)
+            o = tile([P, PACK, width], F32, "o%d" % c)
+            for t in range(PACK):
+                nc.vector.tensor_tensor(o[:, t, :], neg_h[t][:].indirect(entries(n4_t, start, width)), h[t][:, cols], ADD)
+            nc.sync.dma_start(out_rows[:, :, cols], o[:])
+            o_bf = tile([P, PACK * width], BF16, "o_bf%d" % c)
+            interleave(nc.scalar.copy, o_bf, o)
+            o_codes = tile([P, width], I32, "o_codes%d" % c)
+            nc.vector.quantize_mx(out=o_codes[:].bitcast(FP8X4), scales=o_scales[:, cols], in_=o_bf[:])
+            nc.sync.dma_start(out_words[:, cols], o_codes[:])
+        for q in range(4):
+            queue = nc.scalar if q % 2 else nc.sync
+            queue.dma_start(out_2[0, 4 * q : 4 * q + 4, :].bitcast(I32), o_scales[32 * q : 32 * q + 4, :].bitcast(I32))

@@ -21,7 +21,7 @@ P = 128
 PACK = 4
 HALF = H // 2
 CHUNKS = ((0, 256), (256, 128), (384, 128))
-Z_CHUNK = 128
+Z_CHUNKS = ((0, 256), (256, 128), (384, 128))
 
 
 def tile_picked_tokkindadif_none_po_kernel(
@@ -33,8 +33,8 @@ def tile_picked_tokkindadif_none_po_kernel(
         sb = ctx.enter_context(tc.tile_pool(name="sb", bufs=1))
         ps = ctx.enter_context(tc.psum_pool(name="ps", bufs=1))
 
-        def tile(shape, dtype, name):
-            return sb.tile(shape, dtype, name=name, align_bytes=64)
+        def tile(shape, dtype, name, tag=None):
+            return sb.tile(shape, dtype, name=name, tag=tag or name, align_bytes=64)
 
         def load_list(src, name):
             dst = lists.tile([P, 32], U16, name=name)
@@ -47,18 +47,18 @@ def tile_picked_tokkindadif_none_po_kernel(
         def interleave(engine_copy, dst, src):
             engine_copy(
                 dst[:].rearrange("p (c i t) -> p c t i", i=4, t=PACK),
-                src[:].rearrange("p t (c i) -> p c t i", i=4),
+                src.rearrange("p t (c i) -> p c t i", i=4),
             )
 
         xs = tile([P, T], U8, "xs")
         nc.vector.memset(xs[:].bitcast(I32), 0)
         w1s = tile([P, N], U8, "w1s")
-        nc.vector.memset(w1s[:].bitcast(I32), 0)
+        nc.gpsimd.memset(w1s[:].bitcast(I32), 0)
 
         tab_rows = tab.rearrange("(p t) j -> p t j", t=PACK)
         wa_rows = wa.rearrange("(p t) j -> p t j", t=PACK)
         tab_t = [tile([P, H], F32, "tab%d" % t) for t in range(PACK)]
-        wa_raw = [tile([P, PACK, HALF], F32, "wa_raw%d" % u) for u in range(2)]
+        wa_raw = tile([P, PACK, H], F32, "wa_raw")
         xw = tile([P, T], I32, "xw")
         gt_t = tile([P, PACK], F32, "gt_t")
         w1w = tile([P, 2 * N], U8, "w1w")
@@ -66,28 +66,27 @@ def tile_picked_tokkindadif_none_po_kernel(
         n1_t = load_list(n1, "n1_t")
         for t in (0, 1):
             nc.sync.dma_start(tab_t[t][:], tab_rows[:, t, :])
-        for u in range(2):
-            nc.sync.dma_start(wa_raw[u][:], wa_rows[:, :, u * HALF : (u + 1) * HALF])
+        for q in range(4):
+            nc.scalar.dma_start(xs[32 * q : 32 * q + 4, :].bitcast(I32), x_scales[0, 4 * q : 4 * q + 4, :].bitcast(I32))
         offs_t = load_list(offs, "offs_t")
+        nc.sync.dma_start(wa_raw[:], wa_rows)
+        nc.sync.dma_start(tab_t[2][:], tab_rows[:, 2, :])
         nc.sync.dma_start(xw[:], x_words[0].rearrange("p c r -> p (c r)").bitcast(I32))
-        for t in (2, 3):
-            nc.sync.dma_start(tab_t[t][:], tab_rows[:, t, :])
+        nc.sync.dma_start(tab_t[3][:], tab_rows[:, 3, :])
         n3_t = load_list(n3, "n3_t")
         n2_t = load_list(n2, "n2_t")
-        n4_t = load_list(n4, "n4_t")
         nc.sync.dma_start(w1w[:].bitcast(I32), w1_words[0].bitcast(I32))
-        for q in range(4):
-            nc.gpsimd.dma_start(xs[32 * q : 32 * q + 4, :].bitcast(I32), x_scales[0, 4 * q : 4 * q + 4, :].bitcast(I32))
+        n4_t = load_list(n4, "n4_t")
         nc.gpsimd.dma_start(gt_t[:], gt.rearrange("(p t) o -> p (t o)", t=PACK))
         for q in range(4):
             nc.gpsimd.dma_start(w1s[32 * q : 32 * q + 4, :].bitcast(I32), w1_scales[0, 4 * q : 4 * q + 4, :].bitcast(I32))
 
-        a = [tile([P, H], F32, "a%d" % t) for t in range(PACK)]
+        a = [[tile([P, HALF], F32, "a%d_%d" % (t, u)) for u in range(2)] for t in range(PACK)]
         tabg = [tile([P, H], F32, "tabg%d" % t) for t in range(PACK)]
 
         def fetch_n1(t):
             for u in range(2):
-                nc.vector.tensor_copy(a[t][:, u * HALF : (u + 1) * HALF], tab_t[t][:].indirect(entries(n1_t, u * HALF, HALF)))
+                nc.vector.tensor_copy(a[t][u][:], tab_t[t][:].indirect(entries(n1_t, u * HALF, HALF)))
 
         fetch_n1(0)
         fetch_n1(1)
@@ -99,27 +98,21 @@ def tile_picked_tokkindadif_none_po_kernel(
             xsd[:].rearrange("p (t c i) -> p c t i", t=PACK, i=16),
             xsg[:].rearrange("p (c i t) -> p c t i", t=PACK, i=16),
         )
+        fetch_n1(2)
         wa_codes = tile([P, H], U32, "wa_codes")
         wa_scales = tile([P, H], U8, "wa_scales")
         for u in range(2):
             grouped = tile([P, PACK * HALF], BF16, "wa_bf%d" % u)
-            interleave(nc.scalar.copy, grouped, wa_raw[u])
             cols = slice(u * HALF, (u + 1) * HALF)
+            interleave(nc.scalar.copy, grouped, wa_raw[:, :, cols])
             nc.vector.quantize_mx(out=wa_codes[:, cols].bitcast(FP8X4), scales=wa_scales[:, cols], in_=grouped[:])
-        xg = tile([P, S], I32, "xg")
-        nc.vector.tensor_copy(xg[:].bitcast(U32), xw[:].bitcast(U32).indirect(offs_t[:]))
-        xd = tile([P, S], I32, "xd")
-        nc.vector.tensor_copy(
-            xd[:].rearrange("p (t c i) -> p c t i", t=PACK, i=4),
-            xg[:].rearrange("p (c i t) -> p c t i", t=PACK, i=4),
-        )
-        fetch_n1(2)
-        fetch_n1(3)
+        xd = tile([P, S], U32, "xd")
+        nc.vector.tensor_copy(xd[:].rearrange("p (t m) -> p m t", t=PACK), xw[:].bitcast(U32).indirect(offs_t[:]))
 
         y_t = []
         for t in range(PACK):
             cols = slice(t * P, (t + 1) * P)
-            bank = ps.tile([P, H], F32, name="ybank%d" % t)
+            bank = ps.tile([P, H], F32, name="ybank%d" % t, tag="row_bank%d" % t)
             nc.tensor.matmul_mx(
                 out=bank[:], lhsT=xd[:, cols].bitcast(FP8X4), lhsT_scale=xsd[:, cols],
                 rhs=wa_codes[:].bitcast(FP8X4), rhs_scale=wa_scales[:], start=True, stop=True,
@@ -127,49 +120,56 @@ def tile_picked_tokkindadif_none_po_kernel(
             plane = tile([P, H], F32, "y%d" % t)
             nc.scalar.activation(plane[:], bank[:], COPY, scale=gt_t[:, t : t + 1])
             y_t.append(plane)
-
+        fetch_n1(3)
         for t in range(PACK):
             nc.scalar.activation(tabg[t][:], tab_t[t][:], COPY, scale=gt_t[:, t : t + 1])
 
-        w1d = tile([P, 2 * N], U8, "w1d")
+        w1d = tile([P, 2 * N], U8, "w1d", "xw")
+        w1sd = tile([P, N], U8, "w1sd", "tab3")
         nc.vector.tensor_copy(
             w1d[:].rearrange("p (t c i b) -> p c t i b", t=PACK, i=8, b=2),
             w1w[:].rearrange("p (c i t b) -> p c t i b", t=PACK, i=8, b=2),
         )
-        w1sd = tile([P, N], U8, "w1sd")
         nc.vector.tensor_copy(
             w1sd[:].rearrange("p (t c i) -> p c t i", t=PACK, i=16),
             w1s[:].rearrange("p (c i t) -> p c t i", t=PACK, i=16),
         )
-
-        hbank = [ps.tile([P, H], F32, name="hbank%d" % t) for t in range(PACK)]
         neg_h = [tile([P, H], F32, "neg_h%d" % t) for t in range(PACK)]
-        h = [tile([P, H], F32, "h%d" % t) for t in range(PACK)]
-        b = [tile([P, H], F32, "b%d" % t) for t in range(PACK)]
-        width = Z_CHUNK
-        for c, start in enumerate(range(0, H, Z_CHUNK)):
+        h = tile([P, PACK, H], F32, "h")
+        held = []
+        for c, (start, width) in enumerate(Z_CHUNKS):
             cols = slice(start, start + width)
-            z = tile([P, PACK, width], F32, "z%d" % c)
-            if start % HALF == 0:
-                half = slice(start, start + HALF)
-                for t in range(PACK):
-                    nc.vector.tensor_tensor(b[t][:, half], y_t[t][:].indirect(entries(n3_t, start, HALF)), a[t][:, half], MULT)
+            last = start + width == H
+            u, inner = divmod(start, HALF)
+            z = sb.tile([P, PACK, width], F32, name="z%d" % c, tag="z", bufs=1, align_bytes=64)
+            b = [tile([P, width], F32, "b%d_%d" % (c, t), "b%d" % t) for t in range(PACK)]
             for t in range(PACK):
-                nc.vector.tensor_tensor(z[:, t, :], tabg[t][:].indirect(entries(n2_t, start, width)), b[t][:, cols], ADD)
+                nc.vector.tensor_tensor(b[t][:], y_t[t][:].indirect(entries(n3_t, start, width)), a[t][u][:, inner : inner + width], MULT)
+            for t in range(PACK):
+                nc.vector.tensor_tensor(z[:, t, :], tabg[t][:].indirect(entries(n2_t, start, width)), b[t][:], ADD)
             z_bf = tile([P, PACK * width], BF16, "z_bf%d" % c)
-            interleave(nc.vector.tensor_copy if start + width == H else nc.scalar.copy, z_bf, z)
+            interleave(nc.vector.tensor_copy if last else nc.scalar.copy, z_bf, z[:])
             z_codes = tile([P, width], U32, "z_codes%d" % c)
             z_scales = tile([P, width], U8, "z_scales%d" % c)
             nc.vector.quantize_mx(out=z_codes[:].bitcast(FP8X4), scales=z_scales[:], in_=z_bf[:])
+            per_bank = 1 if last else H // width
+            banks = [
+                ps.tile([P, per_bank, width], F32, name="h%d_%d" % (c, g), tag=("row_bank%d" % g) if last else "h%d_%d" % (c, g))
+                for g in range(PACK // per_bank)
+            ]
+            sums = [banks[t // per_bank][:, t % per_bank, :] for t in range(PACK)]
             for t in range(PACK):
                 nc.tensor.matmul_mx(
-                    out=hbank[t][:, cols], lhsT=w1d[:, 2 * P * t : 2 * P * (t + 1)].bitcast(FP4X4),
+                    out=sums[t], lhsT=w1d[:, 2 * P * t : 2 * P * (t + 1)].bitcast(FP4X4),
                     lhsT_scale=w1sd[:, P * t : P * (t + 1)],
                     rhs=z_codes[:].bitcast(FP8X4), rhs_scale=z_scales[:], start=True, stop=True,
                 )
-                nc.scalar.activation(neg_h[t][:, cols], hbank[t][:, cols], COPY, scale=-1.0)
             for t in range(PACK):
-                nc.scalar.copy(h[t][:, cols], hbank[t][:, cols])
+                nc.scalar.activation(neg_h[t][:, cols], sums[t], COPY, scale=-1.0)
+            for g, bank in enumerate(banks):
+                held.append((h[:, g * per_bank : (g + 1) * per_bank, cols], bank))
+        for dst, bank in held:
+            nc.scalar.copy(dst, bank[:])
 
         out_rows = out_0.rearrange("(p t) j -> p t j", t=PACK)
         out_words = out_1[0].rearrange("p c r -> p (c r)").bitcast(I32)
@@ -178,10 +178,10 @@ def tile_picked_tokkindadif_none_po_kernel(
             cols = slice(start, start + width)
             o = tile([P, PACK, width], F32, "o%d" % c)
             for t in range(PACK):
-                nc.vector.tensor_tensor(o[:, t, :], neg_h[t][:].indirect(entries(n4_t, start, width)), h[t][:, cols], ADD)
+                nc.vector.tensor_tensor(o[:, t, :], neg_h[t][:].indirect(entries(n4_t, start, width)), h[:, t, cols], ADD)
             nc.sync.dma_start(out_rows[:, :, cols], o[:])
             o_bf = tile([P, PACK * width], BF16, "o_bf%d" % c)
-            interleave(nc.scalar.copy, o_bf, o)
+            interleave(nc.scalar.copy, o_bf, o[:])
             o_codes = tile([P, width], I32, "o_codes%d" % c)
             nc.vector.quantize_mx(out=o_codes[:].bitcast(FP8X4), scales=o_scales[:, cols], in_=o_bf[:])
             nc.sync.dma_start(out_words[:, cols], o_codes[:])

@@ -20,8 +20,8 @@ ADD = mybir.AluOpType.add
 P = 128
 PACK = 4
 HALF = H // 2
-CHUNKS = ((0, 256), (256, 128), (384, 128))
-Z_CHUNKS = ((0, 256), (256, 128), (384, 128))
+GROUP = 16
+QUADRANTS = 4
 
 
 def tile_picked_tokkindadif_none_po_kernel(
@@ -37,16 +37,25 @@ def tile_picked_tokkindadif_none_po_kernel(
             return sb.tile(shape, dtype, name=name, tag=tag or name, align_bytes=64)
 
         def load_list(src, name):
-            dst = lists.tile([P, 32], U16, name=name)
+            dst = lists.tile([P, S // GROUP], U16, name=name)
             nc.sync.dma_start(dst[:], src)
             return dst
 
         def entries(lst, start, width):
-            return lst[:, start // 16 : (start + width) // 16]
+            return lst[:, start // GROUP : (start + width) // GROUP]
+
+        def scale_rows(plane, q):
+            return plane[32 * q : 32 * q + 4, :].bitcast(I32)
 
         def interleave(engine_copy, dst, src):
             engine_copy(
-                dst[:].rearrange("p (c i t) -> p c t i", i=4, t=PACK),
+                dst.rearrange("p (c i t) -> p c t i", i=4, t=PACK),
+                src.rearrange("p t (c i) -> p c t i", i=4),
+            )
+
+        def interleave_pair(engine_copy, dst, g, src):
+            engine_copy(
+                dst.rearrange("p (c i g t) -> p g c t i", i=4, g=2, t=2)[:, g],
                 src.rearrange("p t (c i) -> p c t i", i=4),
             )
 
@@ -57,39 +66,41 @@ def tile_picked_tokkindadif_none_po_kernel(
 
         tab_rows = tab.rearrange("(p t) j -> p t j", t=PACK)
         wa_rows = wa.rearrange("(p t) j -> p t j", t=PACK)
-        tab_t = [tile([P, H], F32, "tab%d" % t) for t in range(PACK)]
+        wide = [tile([P, 2 * H], F32, "wide%d" % t) for t in range(PACK)]
+        for t in range(PACK):
+            nc.vector.memset(wide[t][:, H:], 0.0)
         wa_raw = tile([P, PACK, H], F32, "wa_raw")
         xw = tile([P, T], I32, "xw")
         gt_t = tile([P, PACK], F32, "gt_t")
         w1w = tile([P, 2 * N], U8, "w1w")
 
+        last = PACK - 1
         n1_t = load_list(n1, "n1_t")
-        for t in (0, 1):
-            nc.sync.dma_start(tab_t[t][:], tab_rows[:, t, :])
-        for q in range(4):
-            nc.scalar.dma_start(xs[32 * q : 32 * q + 4, :].bitcast(I32), x_scales[0, 4 * q : 4 * q + 4, :].bitcast(I32))
-        offs_t = load_list(offs, "offs_t")
+        for t in range(last):
+            nc.sync.dma_start(wide[t][:, :H], tab_rows[:, t, :])
+        nc.scalar.dma_start(gt_t[:], gt.rearrange("(p t) o -> p (t o)", t=PACK))
+        for q in range(QUADRANTS):
+            nc.scalar.dma_start(scale_rows(xs, q), x_scales[0, 4 * q : 4 * q + 4, :].bitcast(I32))
         nc.sync.dma_start(wa_raw[:], wa_rows)
-        nc.sync.dma_start(tab_t[2][:], tab_rows[:, 2, :])
+        offs_t = load_list(offs, "offs_t")
         nc.sync.dma_start(xw[:], x_words[0].rearrange("p c r -> p (c r)").bitcast(I32))
-        nc.sync.dma_start(tab_t[3][:], tab_rows[:, 3, :])
+        nc.sync.dma_start(wide[last][:, :H], tab_rows[:, last, :])
         n3_t = load_list(n3, "n3_t")
         n2_t = load_list(n2, "n2_t")
-        nc.sync.dma_start(w1w[:].bitcast(I32), w1_words[0].bitcast(I32))
+        nc.gpsimd.dma_start(w1w[:].bitcast(I32), w1_words[0].bitcast(I32))
+        for q in range(QUADRANTS):
+            nc.gpsimd.dma_start(scale_rows(w1s, q), w1_scales[0, 4 * q : 4 * q + 4, :].bitcast(I32))
         n4_t = load_list(n4, "n4_t")
-        nc.gpsimd.dma_start(gt_t[:], gt.rearrange("(p t) o -> p (t o)", t=PACK))
-        for q in range(4):
-            nc.gpsimd.dma_start(w1s[32 * q : 32 * q + 4, :].bitcast(I32), w1_scales[0, 4 * q : 4 * q + 4, :].bitcast(I32))
 
-        a = [[tile([P, HALF], F32, "a%d_%d" % (t, u)) for u in range(2)] for t in range(PACK)]
+        a = [tile([P, H], F32, "a%d" % t) for t in range(PACK)]
         tabg = [tile([P, H], F32, "tabg%d" % t) for t in range(PACK)]
 
-        def fetch_n1(t):
-            for u in range(2):
-                nc.vector.tensor_copy(a[t][u][:], tab_t[t][:].indirect(entries(n1_t, u * HALF, HALF)))
+        def use_tab_plane(t):
+            nc.vector.tensor_copy(a[t][:], wide[t][:].indirect(n1_t[:]))
+            nc.scalar.activation(tabg[t][:], wide[t][:, :H], COPY, scale=gt_t[:, t : t + 1])
 
-        fetch_n1(0)
-        fetch_n1(1)
+        for t in range(last):
+            use_tab_plane(t)
 
         xsg = tile([P, S], U8, "xsg")
         nc.vector.tensor_copy(xsg[:], xs[:].indirect(offs_t[:]))
@@ -98,34 +109,33 @@ def tile_picked_tokkindadif_none_po_kernel(
             xsd[:].rearrange("p (t c i) -> p c t i", t=PACK, i=16),
             xsg[:].rearrange("p (c i t) -> p c t i", t=PACK, i=16),
         )
-        fetch_n1(2)
         wa_codes = tile([P, H], U32, "wa_codes")
         wa_scales = tile([P, H], U8, "wa_scales")
-        for u in range(2):
-            grouped = tile([P, PACK * HALF], BF16, "wa_bf%d" % u)
-            cols = slice(u * HALF, (u + 1) * HALF)
+        wa_bf = tile([P, PACK * HALF], BF16, "wa_bf")
+        for start, grouped in ((0, wa_bf[:]), (HALF, a[last][:].bitcast(BF16))):
+            cols = slice(start, start + HALF)
             interleave(nc.scalar.copy, grouped, wa_raw[:, :, cols])
-            nc.vector.quantize_mx(out=wa_codes[:, cols].bitcast(FP8X4), scales=wa_scales[:, cols], in_=grouped[:])
-        xd = tile([P, S], U32, "xd")
-        nc.vector.tensor_copy(xd[:].rearrange("p (t m) -> p m t", t=PACK), xw[:].bitcast(U32).indirect(offs_t[:]))
+            nc.vector.quantize_mx(out=wa_codes[:, cols].bitcast(FP8X4), scales=wa_scales[:, cols], in_=grouped)
+        xg = tile([P, S], I32, "xg")
+        nc.vector.tensor_copy(xg[:].bitcast(U32), xw[:].bitcast(U32).indirect(offs_t[:]))
+        xd = tile([P, S], I32, "xd")
+        nc.vector.tensor_copy(
+            xd[:].rearrange("p (t c i) -> p c t i", t=PACK, i=4),
+            xg[:].rearrange("p (c i t) -> p c t i", t=PACK, i=4),
+        )
+        use_tab_plane(last)
 
-        y_t = []
         for t in range(PACK):
             cols = slice(t * P, (t + 1) * P)
-            bank = ps.tile([P, H], F32, name="ybank%d" % t, tag="row_bank%d" % t)
+            bank = ps.tile([P, H], F32, name="y_bank%d" % t, tag="row_bank%d" % t)
             nc.tensor.matmul_mx(
                 out=bank[:], lhsT=xd[:, cols].bitcast(FP8X4), lhsT_scale=xsd[:, cols],
                 rhs=wa_codes[:].bitcast(FP8X4), rhs_scale=wa_scales[:], start=True, stop=True,
             )
-            plane = tile([P, H], F32, "y%d" % t)
-            nc.scalar.activation(plane[:], bank[:], COPY, scale=gt_t[:, t : t + 1])
-            y_t.append(plane)
-        fetch_n1(3)
-        for t in range(PACK):
-            nc.scalar.activation(tabg[t][:], tab_t[t][:], COPY, scale=gt_t[:, t : t + 1])
+            nc.scalar.activation(wide[t][:, :H], bank[:], COPY, scale=gt_t[:, t : t + 1])
 
         w1d = tile([P, 2 * N], U8, "w1d", "xw")
-        w1sd = tile([P, N], U8, "w1sd", "tab3")
+        w1sd = tile([P, N], U8, "w1sd", "xg")
         nc.vector.tensor_copy(
             w1d[:].rearrange("p (t c i b) -> p c t i b", t=PACK, i=8, b=2),
             w1w[:].rearrange("p (c i t b) -> p c t i b", t=PACK, i=8, b=2),
@@ -134,57 +144,74 @@ def tile_picked_tokkindadif_none_po_kernel(
             w1sd[:].rearrange("p (t c i) -> p c t i", t=PACK, i=16),
             w1s[:].rearrange("p (c i t) -> p c t i", t=PACK, i=16),
         )
+
+        halves = [slice(0, HALF), slice(HALF, H)]
         neg_h = [tile([P, H], F32, "neg_h%d" % t) for t in range(PACK)]
         h = tile([P, PACK, H], F32, "h")
-        held = []
-        for c, (start, width) in enumerate(Z_CHUNKS):
-            cols = slice(start, start + width)
-            last = start + width == H
-            u, inner = divmod(start, HALF)
-            z = sb.tile([P, PACK, width], F32, name="z%d" % c, tag="z", bufs=1, align_bytes=64)
-            b = [tile([P, width], F32, "b%d_%d" % (c, t), "b%d" % t) for t in range(PACK)]
-            for t in range(PACK):
-                nc.vector.tensor_tensor(b[t][:], y_t[t][:].indirect(entries(n3_t, start, width)), a[t][u][:, inner : inner + width], MULT)
-            for t in range(PACK):
-                nc.vector.tensor_tensor(z[:, t, :], tabg[t][:].indirect(entries(n2_t, start, width)), b[t][:], ADD)
-            z_bf = tile([P, PACK * width], BF16, "z_bf%d" % c)
-            interleave(nc.vector.tensor_copy if last else nc.scalar.copy, z_bf, z[:])
-            z_codes = tile([P, width], U32, "z_codes%d" % c)
-            z_scales = tile([P, width], U8, "z_scales%d" % c)
+        b = [tile([P, H], F32, "b%d" % t) for t in range(PACK)]
+
+        def add_term(dst, u, t):
+            nc.vector.tensor_tensor(dst, tabg[t][:].indirect(entries(n2_t, u * HALF, HALF)), b[t][:, halves[u]], ADD)
+
+        def second_product(u, z_bf, sums, planes):
+            z_codes = tile([P, HALF], U32, "z_codes%d" % u)
+            z_scales = tile([P, HALF], U8, "z_scales%d" % u)
             nc.vector.quantize_mx(out=z_codes[:].bitcast(FP8X4), scales=z_scales[:], in_=z_bf[:])
-            per_bank = 1 if last else H // width
-            banks = [
-                ps.tile([P, per_bank, width], F32, name="h%d_%d" % (c, g), tag=("row_bank%d" % g) if last else "h%d_%d" % (c, g))
-                for g in range(PACK // per_bank)
-            ]
-            sums = [banks[t // per_bank][:, t % per_bank, :] for t in range(PACK)]
-            for t in range(PACK):
+            for t in planes:
                 nc.tensor.matmul_mx(
                     out=sums[t], lhsT=w1d[:, 2 * P * t : 2 * P * (t + 1)].bitcast(FP4X4),
                     lhsT_scale=w1sd[:, P * t : P * (t + 1)],
                     rhs=z_codes[:].bitcast(FP8X4), rhs_scale=z_scales[:], start=True, stop=True,
                 )
-            for t in range(PACK):
-                nc.scalar.activation(neg_h[t][:, cols], sums[t], COPY, scale=-1.0)
-            for g, bank in enumerate(banks):
-                held.append((h[:, g * per_bank : (g + 1) * per_bank, cols], bank))
-        for dst, bank in held:
-            nc.scalar.copy(dst, bank[:])
+
+        z = tile([P, PACK, HALF], F32, "z")
+        for t in range(PACK):
+            nc.vector.tensor_tensor(b[t][:], wide[t][:].indirect(n3_t[:]), a[t][:], MULT)
+            if t > 0:
+                add_term(z[:, t - 1, :], 0, t - 1)
+        add_term(z[:, last, :], 0, last)
+        z_bf = tile([P, PACK * HALF], BF16, "z_bf0")
+        interleave(nc.scalar.copy, z_bf[:], z[:])
+        banks = [ps.tile([P, 2, HALF], F32, name="h_pair%d" % g) for g in range(2)]
+        second_product(0, z_bf, [banks[t // 2][:, t % 2, :] for t in range(PACK)], range(PACK))
+
+        z_pair = [z[:, 0:2, :], a[last][:].rearrange("p (t w) -> p t w", t=2)]
+        z_bf = tile([P, PACK * HALF], BF16, "z_bf1")
+        for g, engine_copy in ((1, nc.scalar.copy), (0, nc.vector.tensor_copy)):
+            for t in (2 * g, 2 * g + 1):
+                add_term(z_pair[g][:, t % 2, :], 1, t)
+            interleave_pair(engine_copy, z_bf[:], g, z_pair[g])
+        for t in range(PACK):
+            nc.scalar.activation(neg_h[t][:, halves[0]], banks[t // 2][:, t % 2, :], COPY, scale=-1.0)
+        for g in range(2):
+            nc.scalar.copy(h[:, 2 * g : 2 * g + 2, halves[0]], banks[g][:])
+
+        order = (0, 2, 1, 3)
+        sums = [ps.tile([P, HALF], F32, name="h_row%d" % t, tag="row_bank%d" % t)[:] for t in range(PACK)]
+        second_product(1, z_bf, sums, order)
+        nc.vector.tensor_scalar_mul(neg_h[order[0]][:, halves[1]], sums[order[0]], -1.0)
+        for t in order[1:]:
+            nc.scalar.activation(neg_h[t][:, halves[1]], sums[t], COPY, scale=-1.0)
+        for t in order:
+            nc.scalar.copy(h[:, t, halves[1]], sums[t])
 
         out_rows = out_0.rearrange("(p t) j -> p t j", t=PACK)
         out_words = out_1[0].rearrange("p c r -> p (c r)").bitcast(I32)
         o_scales = tile([P, H], U8, "o_scales")
-        for c, (start, width) in enumerate(CHUNKS):
-            cols = slice(start, start + width)
-            o = tile([P, PACK, width], F32, "o%d" % c)
-            for t in range(PACK):
-                nc.vector.tensor_tensor(o[:, t, :], neg_h[t][:].indirect(entries(n4_t, start, width)), h[:, t, cols], ADD)
-            nc.sync.dma_start(out_rows[:, :, cols], o[:])
-            o_bf = tile([P, PACK * width], BF16, "o_bf%d" % c)
-            interleave(nc.scalar.copy, o_bf, o[:])
-            o_codes = tile([P, width], I32, "o_codes%d" % c)
-            nc.vector.quantize_mx(out=o_codes[:].bitcast(FP8X4), scales=o_scales[:, cols], in_=o_bf[:])
-            nc.sync.dma_start(out_words[:, cols], o_codes[:])
-        for q in range(4):
-            queue = nc.scalar if q % 2 else nc.sync
-            queue.dma_start(out_2[0, 4 * q : 4 * q + 4, :].bitcast(I32), o_scales[32 * q : 32 * q + 4, :].bitcast(I32))
+        o = [[tile([P, 2, HALF], F32, "o%d_%d" % (u, g)) for g in range(2)] for u in range(2)]
+        for u in range(2):
+            for t in order:
+                looked_up = neg_h[t][:].indirect(entries(n4_t, u * HALF, HALF))
+                nc.vector.tensor_tensor(o[u][t // 2][:, t % 2, :], looked_up, h[:, t, halves[u]], ADD)
+        for u in range(2):
+            o_bf = tile([P, PACK * HALF], BF16, "o_bf%d" % u)
+            for g in range(2):
+                nc.sync.dma_start(out_rows[:, 2 * g : 2 * g + 2, halves[u]], o[u][g][:])
+                engine_copy = nc.vector.tensor_copy if (u, g) == (1, 1) else nc.scalar.copy
+                interleave_pair(engine_copy, o_bf[:], g, o[u][g][:])
+            o_codes = tile([P, HALF], I32, "o_codes%d" % u)
+            nc.vector.quantize_mx(out=o_codes[:].bitcast(FP8X4), scales=o_scales[:, halves[u]], in_=o_bf[:])
+            nc.sync.dma_start(out_words[:, halves[u]], o_codes[:])
+        for q in range(QUADRANTS):
+            queue = nc.sync if q == QUADRANTS - 1 else nc.scalar
+            queue.dma_start(out_2[0, 4 * q : 4 * q + 4, :].bitcast(I32), scale_rows(o_scales, q))

from contextlib import ExitStack

import concourse.mybir as mybir

K, T, S, N, H = 512, 2048, 512, 512, 512
FLOPS = 2 * K * S * H + 2 * S * N * H

F32 = mybir.dt.float32
BF16 = mybir.dt.bfloat16
I32 = mybir.dt.int32
U32 = mybir.dt.uint32
U16 = mybir.dt.uint16
U8 = mybir.dt.uint8
FP8X4 = mybir.dt.float8_e4m3fn_x4
FP4X4 = mybir.dt.float4_e2m1fn_x4
COPY = mybir.ActivationFunctionType.Copy
MULT = mybir.AluOpType.mult
ADD = mybir.AluOpType.add

P = 128
PACK = 4
HALF = H // 2
GROUP = 16
QUADRANTS = 4


def tile_picked_tokkindadif_none_po_kernel(
    tc, x_words, x_scales, wa, tab, gt, w1_words, w1_scales, offs, n1, n2, n3, n4, out_0, out_1, out_2
):
    nc = tc.nc
    with ExitStack() as ctx:
        lists = ctx.enter_context(tc.tile_pool(name="lists", bufs=1))
        sb = ctx.enter_context(tc.tile_pool(name="sb", bufs=1))
        ps = ctx.enter_context(tc.psum_pool(name="ps", bufs=1))

        def tile(shape, dtype, name, tag=None):
            return sb.tile(shape, dtype, name=name, tag=tag or name, align_bytes=64)

        def load_list(src, name):
            dst = lists.tile([P, S // GROUP], U16, name=name)
            nc.sync.dma_start(dst[:], src)
            return dst

        def entries(lst, start, width):
            return lst[:, start // GROUP : (start + width) // GROUP]

        def scale_rows(plane, q):
            return plane[32 * q : 32 * q + 4, :].bitcast(I32)

        def interleave(engine_copy, dst, src):
            engine_copy(
                dst.rearrange("p (c i t) -> p c t i", i=4, t=PACK),
                src.rearrange("p t (c i) -> p c t i", i=4),
            )

        def interleave_pair(engine_copy, dst, g, src):
            engine_copy(
                dst.rearrange("p (c i g t) -> p g c t i", i=4, g=2, t=2)[:, g],
                src.rearrange("p t (c i) -> p c t i", i=4),
            )

        xs = tile([P, T], U8, "xs")
        nc.vector.memset(xs[:].bitcast(I32), 0)
        w1s = tile([P, N], U8, "w1s")
        nc.gpsimd.memset(w1s[:].bitcast(I32), 0)

        tab_rows = tab.rearrange("(p t) j -> p t j", t=PACK)
        wa_rows = wa.rearrange("(p t) j -> p t j", t=PACK)
        wide = [tile([P, 2 * H], F32, "wide%d" % t) for t in range(PACK)]
        for t in range(PACK):
            nc.vector.memset(wide[t][:, H:], 0.0)
        wa_raw = tile([P, PACK, H], F32, "wa_raw")
        xw = tile([P, T], I32, "xw")
        gt_t = tile([P, PACK], F32, "gt_t")
        w1w = tile([P, 2 * N], U8, "w1w")

        last = PACK - 1
        n1_t = load_list(n1, "n1_t")
        for t in range(last):
            nc.sync.dma_start(wide[t][:, :H], tab_rows[:, t, :])
        nc.scalar.dma_start(gt_t[:], gt.rearrange("(p t) o -> p (t o)", t=PACK))
        for q in range(QUADRANTS):
            nc.scalar.dma_start(scale_rows(xs, q), x_scales[0, 4 * q : 4 * q + 4, :].bitcast(I32))
        nc.sync.dma_start(wa_raw[:], wa_rows)
        offs_t = load_list(offs, "offs_t")
        nc.sync.dma_start(xw[:], x_words[0].rearrange("p c r -> p (c r)").bitcast(I32))
        nc.sync.dma_start(wide[last][:, :H], tab_rows[:, last, :])
        n3_t = load_list(n3, "n3_t")
        n2_t = load_list(n2, "n2_t")
        nc.gpsimd.dma_start(w1w[:].bitcast(I32), w1_words[0].bitcast(I32))
        for q in range(QUADRANTS):
            nc.gpsimd.dma_start(scale_rows(w1s, q), w1_scales[0, 4 * q : 4 * q + 4, :].bitcast(I32))
        n4_t = load_list(n4, "n4_t")

        a = [tile([P, H], F32, "a%d" % t) for t in range(PACK)]
        tabg = [tile([P, H], F32, "tabg%d" % t) for t in range(PACK)]

        def use_tab_plane(t):
            nc.vector.tensor_copy(a[t][:], wide[t][:].indirect(n1_t[:]))
            nc.scalar.activation(tabg[t][:], wide[t][:, :H], COPY, scale=gt_t[:, t : t + 1])

        for t in range(last):
            use_tab_plane(t)

        xsg = tile([P, S], U8, "xsg")
        nc.vector.tensor_copy(xsg[:], xs[:].indirect(offs_t[:]))
        xsd = tile([P, S], U8, "xsd")
        nc.vector.tensor_copy(
            xsd[:].rearrange("p (t c i) -> p c t i", t=PACK, i=16),
            xsg[:].rearrange("p (c i t) -> p c t i", t=PACK, i=16),
        )
        wa_codes = tile([P, H], U32, "wa_codes")
        wa_scales = tile([P, H], U8, "wa_scales")
        wa_bf = tile([P, PACK * HALF], BF16, "wa_bf")
        for start, grouped in ((0, wa_bf[:]), (HALF, a[last][:].bitcast(BF16))):
            cols = slice(start, start + HALF)
            interleave(nc.scalar.copy, grouped, wa_raw[:, :, cols])
            nc.vector.quantize_mx(out=wa_codes[:, cols].bitcast(FP8X4), scales=wa_scales[:, cols], in_=grouped)
        xg = tile([P, S], I32, "xg")
        nc.vector.tensor_copy(xg[:].bitcast(U32), xw[:].bitcast(U32).indirect(offs_t[:]))
        xd = tile([P, S], I32, "xd")
        nc.vector.tensor_copy(
            xd[:].rearrange("p (t c i) -> p c t i", t=PACK, i=4),
            xg[:].rearrange("p (c i t) -> p c t i", t=PACK, i=4),
        )
        use_tab_plane(last)

        for t in range(PACK):
            cols = slice(t * P, (t + 1) * P)
            bank = ps.tile([P, H], F32, name="y_bank%d" % t, tag="row_bank%d" % t)
            nc.tensor.matmul_mx(
                out=bank[:], lhsT=xd[:, cols].bitcast(FP8X4), lhsT_scale=xsd[:, cols],
                rhs=wa_codes[:].bitcast(FP8X4), rhs_scale=wa_scales[:], start=True, stop=True,
            )
            nc.scalar.activation(wide[t][:, :H], bank[:], COPY, scale=gt_t[:, t : t + 1])

        w1d = tile([P, 2 * N], U8, "w1d", "xw")
        w1sd = tile([P, N], U8, "w1sd", "xg")
        nc.vector.tensor_copy(
            w1d[:].rearrange("p (t c i b) -> p c t i b", t=PACK, i=8, b=2),
            w1w[:].rearrange("p (c i t b) -> p c t i b", t=PACK, i=8, b=2),
        )
        nc.vector.tensor_copy(
            w1sd[:].rearrange("p (t c i) -> p c t i", t=PACK, i=16),
            w1s[:].rearrange("p (c i t) -> p c t i", t=PACK, i=16),
        )

        halves = [slice(0, HALF), slice(HALF, H)]
        neg_h = [tile([P, H], F32, "neg_h%d" % t) for t in range(PACK)]
        h = tile([P, PACK, H], F32, "h")
        b = [tile([P, H], F32, "b%d" % t) for t in range(PACK)]

        def add_term(dst, u, t):
            nc.vector.tensor_tensor(dst, tabg[t][:].indirect(entries(n2_t, u * HALF, HALF)), b[t][:, halves[u]], ADD)

        def second_product(u, z_bf, sums, planes):
            z_codes = tile([P, HALF], U32, "z_codes%d" % u)
            z_scales = tile([P, HALF], U8, "z_scales%d" % u)
            nc.vector.quantize_mx(out=z_codes[:].bitcast(FP8X4), scales=z_scales[:], in_=z_bf[:])
            for t in planes:
                nc.tensor.matmul_mx(
                    out=sums[t], lhsT=w1d[:, 2 * P * t : 2 * P * (t + 1)].bitcast(FP4X4),
                    lhsT_scale=w1sd[:, P * t : P * (t + 1)],
                    rhs=z_codes[:].bitcast(FP8X4), rhs_scale=z_scales[:], start=True, stop=True,
                )

        z = tile([P, PACK, HALF], F32, "z")
        for t in range(PACK):
            nc.vector.tensor_tensor(b[t][:], wide[t][:].indirect(n3_t[:]), a[t][:], MULT)
            if t > 0:
                add_term(z[:, t - 1, :], 0, t - 1)
        add_term(z[:, last, :], 0, last)
        z_bf = tile([P, PACK * HALF], BF16, "z_bf0")
        interleave(nc.scalar.copy, z_bf[:], z[:])
        banks = [ps.tile([P, 2, HALF], F32, name="h_pair%d" % g) for g in range(2)]
        second_product(0, z_bf, [banks[t // 2][:, t % 2, :] for t in range(PACK)], range(PACK))

        z_pair = [z[:, 0:2, :], a[last][:].rearrange("p (t w) -> p t w", t=2)]
        z_bf = tile([P, PACK * HALF], BF16, "z_bf1")
        for g, engine_copy in ((1, nc.scalar.copy), (0, nc.vector.tensor_copy)):
            for t in (2 * g, 2 * g + 1):
                add_term(z_pair[g][:, t % 2, :], 1, t)
            interleave_pair(engine_copy, z_bf[:], g, z_pair[g])
        for t in range(PACK):
            nc.scalar.activation(neg_h[t][:, halves[0]], banks[t // 2][:, t % 2, :], COPY, scale=-1.0)
        for g in range(2):
            nc.scalar.copy(h[:, 2 * g : 2 * g + 2, halves[0]], banks[g][:])

        order = (0, 2, 1, 3)
        sums = [ps.tile([P, HALF], F32, name="h_row%d" % t, tag="row_bank%d" % t)[:] for t in range(PACK)]
        second_product(1, z_bf, sums, order)
        nc.vector.tensor_scalar_mul(neg_h[order[0]][:, halves[1]], sums[order[0]], -1.0)
        for t in order[1:]:
            nc.scalar.activation(neg_h[t][:, halves[1]], sums[t], COPY, scale=-1.0)
        for t in order:
            nc.scalar.copy(h[:, t, halves[1]], sums[t])

        out_rows = out_0.rearrange("(p t) j -> p t j", t=PACK)
        out_words = out_1[0].rearrange("p c r -> p (c r)").bitcast(I32)
        o_scales = tile([P, H], U8, "o_scales")
        o = [[tile([P, 2, HALF], F32, "o%d_%d" % (u, g)) for g in range(2)] for u in range(2)]
        for u in range(2):
            for t in order:
                looked_up = neg_h[t][:].indirect(entries(n4_t, u * HALF, HALF))
                nc.vector.tensor_tensor(o[u][t // 2][:, t % 2, :], looked_up, h[:, t, halves[u]], ADD)
        for u in range(2):
            o_bf = tile([P, PACK * HALF], BF16, "o_bf%d" % u)
            for g in range(2):
                nc.sync.dma_start(out_rows[:, 2 * g : 2 * g + 2, halves[u]], o[u][g][:])
                engine_copy = nc.vector.tensor_copy if (u, g) == (1, 1) else nc.scalar.copy
                interleave_pair(engine_copy, o_bf[:], g, o[u][g][:])
            o_codes = tile([P, HALF], I32, "o_codes%d" % u)
            nc.vector.quantize_mx(out=o_codes[:].bitcast(FP8X4), scales=o_scales[:, halves[u]], in_=o_bf[:])
            nc.sync.dma_start(out_words[:, halves[u]], o_codes[:])
        for q in range(QUADRANTS):
            queue = nc.sync if q == QUADRANTS - 1 else nc.scalar
            queue.dma_start(out_2[0, 4 * q : 4 * q + 4, :].bitcast(I32), scale_rows(o_scales, q))
